import numpy as np, ml_dtypes
CORES = [3,5,43,45,51,53,67,69,75,77,83,85,91,93,115,117]
N = 16
V, K = 256, 4
T = V * K; R = V
CAPP = 256
def entries(a): return a.T.reshape(-1)
def pack(v, P): return np.ascontiguousarray(np.asarray(v, np.int32).reshape(-1, P).T)
def lists(rng, how):
    I = rng.integers(0, N * R, (N, T))
    O = np.stack([rng.permutation(np.repeat(np.arange(N), CAPP))[:T] for r in range(N)])
    if how == "full": O = np.stack([rng.permutation(np.repeat(rng.permutation(N)[:T // CAPP], CAPP)) for r in range(N)])
    I = R * O + rng.integers(0, R, (N, T))
    if how == "alike": I = R * O + rng.integers(0, R, (N, 1))
    if how == "edge": I = R * O + np.where(rng.random((N, T)) < 0.5, 0, R - 1)
    if how == "sorted": I = np.sort(I, axis=1)
    return {"nb": np.stack([pack(I[r], 16) for r in range(N)])}
def setup_inputs(rng):
    w = (rng.standard_normal((128, 128), dtype=np.float32) / 16).astype(ml_dtypes.bfloat16)
    return dict({"x": rng.standard_normal((N, 128, V), dtype=np.float32).astype(ml_dtypes.bfloat16), "w": np.broadcast_to(w, (N, 128, 128)).copy()}, **lists(rng, "uniform"))
def setup_inputs_alike(rng):
    d = setup_inputs(rng); d.update(lists(rng, "alike"))
    for k in ("x",): d[k] = (d[k].astype(np.float32) * 1024.0).astype(d[k].dtype)
    return d
def setup_inputs_edge(rng):
    d = setup_inputs(rng); d.update(lists(rng, "edge"))
    for k in ("x",): d[k] = (d[k].astype(np.float32) * (1 / 1024.0)).astype(d[k].dtype)
    return d
def setup_inputs_full(rng):
    d = setup_inputs(rng); d.update(lists(rng, "full"))
    return d
def setup_inputs_sorted(rng):
    d = setup_inputs(rng); d.update(lists(rng, "sorted"))
    return d
def check_inputs(x):
    bad = []
    if x["nb"].min() < 0 or x["nb"].max() >= N * V: bad.append("nb out of range")
    if max(int(np.bincount(entries(a) // V, minlength=N).max()) for a in x["nb"]) > CAPP: bad.append("more than CAPP entries of a list point into one rank's part")
    if not all(np.array_equal(a, x["w"][0]) for a in x["w"]): bad.append("w isn't alike on all ranks")
    return bad
def reference(x, w, nb):
    X, W = x.astype(np.float64), w.astype(np.float64)
    A = np.concatenate(list(X), axis=1)
    return {"y": np.stack([np.maximum(W[r].T @ (X[r] + A[:, entries(nb[r])].reshape(128, V, K).sum(axis=2)), 0.0) for r in range(N)]).astype(ml_dtypes.bfloat16)}

@@ -1,0 +1,200 @@
+from concourse.bass import DstId, RemoteDMATransfer
+from concourse.mybir import AluOpType, ActivationFunctionType
+
+V = 256
+NR = 16
+NQ = 4
+ND = 2
+LIM = 7
+NSIM = 128
+
+SCRATCH = {
+    "win": ("sbuf", [128, NR * V], "bfloat16"),
+    "wsb": ("sbuf", [128, 128], "bfloat16"),
+    "nbi": ("sbuf", [128, 64], "int32"),
+    "off": ("sbuf", [128, 64], "uint16"),
+    "gat": ("sbuf", [128, 4 * V], "bfloat16"),
+    "ysb": ("sbuf", [128, V], "bfloat16"),
+    "ps0": ("psum", [128, 512], "float32"),
+    "ps1": ("psum", [128, 512], "float32"),
+    "ps2": ("psum", [128, 512], "float32"),
+    "ps3": ("psum", [128, 512], "float32"),
+}
+SEMAPHORES = ["a%d" % u for u in range(NR)] + ["ldx", "ldw", "ldn", "offr", "sent", "rl", "st"] + \
+             ["g%d" % q for q in range(NQ)] + ["m%d" % q for q in range(NQ)]
+
+
+def _bits(m):
+    return bin(m).count("1")
+
+
+def make_plan(ranks, topo):
+    chips = []
+    for c in ranks:
+        if topo.chip(c) not in chips:
+            chips.append(topo.chip(c))
+    on = dict((ch, [c for c in ranks if topo.chip(c) == ch]) for ch in chips)
+    unit = dict((c, i) for i, c in enumerate(ranks))
+    n = len(chips)
+
+    def can(w, b):
+        return all(topo.may_write(w, d) for d in on[b])
+
+    first = {}
+    fwd = {}
+    steps = {}
+    for i, a in enumerate(chips):
+        others = [chips[(i + k) % n] for k in range(1, n)]
+        mine = on[a]
+        got = dict((w, []) for w in mine)
+        free = []
+        for o in mine:
+            for b in others:
+                able = [w for w in mine if can(w, b)]
+                if len(able) == 1:
+                    got[able[0]].append((o, b))
+                else:
+                    free.append((o, b))
+        free.sort(key=lambda t: len(got[t[0]]))
+        for o, b in free:
+            w = min(mine, key=lambda x: (len(got[x]), x != o))
+            got[w].append((o, b))
+        helpers = [c for c in range(NSIM) if topo.chip(c) == a and c not in ranks and all(can(c, b) for b in others)]
+        handed = dict((o, []) for o in mine)
+        for w in mine:
+            while len(got[w]) > LIM and helpers:
+                k = max(j for j, t in enumerate(got[w]) if t[0] != w)
+                o, b = got[w].pop(k)
+                h = helpers.pop()
+                handed[o].append(h)
+                steps[h] = [(unit[o], list(on[b]), "off")]
+        for w in mine:
+            own = [t for t in got[w] if t[0] == w]
+            oth = [t for t in got[w] if t[0] != w]
+            seq = own + oth
+            pos = 0
+            lists = {}
+            for j, (o, b) in enumerate(seq):
+                if o != w:
+                    pos = max(pos, 2)
+                if j >= len(seq) - ND:
+                    d = list(on[b])
+                    pos += len(d)
+                else:
+                    same = [r for r in on[b] if topo.die(r) == topo.die(w)]
+                    e = same[0] if same else on[b][0]
+                    d = [e]
+                    pos += 1
+                    fwd.setdefault(e, []).append((pos, unit[o]))
+                lists.setdefault(o, []).extend(d)
+            partners = [p for p in mine if p != w]
+            s_on = (unit[w], handed[w] + partners, "on")
+            s_off = (unit[w], lists.get(w, []), "off")
+            s = [s_on, s_off] if handed[w] else [s_off, s_on]
+            for o in mine:
+                if o != w and lists.get(o):
+                    s.append((unit[o], lists[o], "off"))
+            first[w] = [t for t in s if t[1]]
+    for w in ranks:
+        partners = [p for p in on[topo.chip(w)] if p != w]
+        steps[w] = first[w] + [(u, partners, "on") for _, u in sorted(fwd.get(w, []))]
+    return steps
+
+
+def masks(core, topo):
+    far = [c for c in range(NSIM) if topo.chip(c) != topo.chip(core)][0]
+    near = [c for c in range(NSIM) if topo.chip(c) == topo.chip(core) and c != core][0]
+    off = topo.mask(core, far)
+    return {"off": off, "on": topo.mask(core, near) & ~off}
+
+
+def rank_program(g, core, T, topo):
+    ranks = list(T.cores)
+    plan = make_plan(ranks, topo)
+    if core not in plan:
+        return
+    rank = T.rank_of(core)
+    sem = T.sem
+
+    lands = {}
+    for src, st in plan.items():
+        mk = masks(src, topo)
+        for u, dsts, kind in st:
+            if core in dsts:
+                lands[u] = _bits(mk[kind])
+
+    def slot(u):
+        return T.win[:, u * V:(u + 1) * V]
+
+    if rank is not None:
+        g.sync.dma_start(slot(rank), T.x[:]).then_inc(sem.ldx, 16)
+        g.scalar.dma_start(T.wsb[:], T.w[:]).then_inc(sem.ldw, 16)
+        for k in range(8):
+            q = g.sync if k % 2 == 0 else g.scalar
+            q.dma_start(T.nbi[16 * k:16 * k + 16, :], T.nb[:]).then_inc(sem.ldn, 16)
+        g.wait_ge(sem.ldx, 16)
+
+    mk = masks(core, topo)
+    sent = 0
+    waited = set()
+    for u, dsts, kind in plan[core]:
+        if u != rank and u not in waited:
+            g.wait_ge(sem["a%d" % u], lands[u])
+            waited.add(u)
+        ids = []
+        for d in dsts:
+            rid, pid, _ = topo.addr(d)
+            ids.append(DstId(rid=rid, pnc=pid))
+        t = RemoteDMATransfer(dst_ids=ids, dma_engine_mask=mk[kind], remote_sem=sem["a%d" % u],
+                              srcs=[slot(u)], dsts=[slot(u) for _ in dsts], alu_op=0)
+        g.remote_dma_fused([t], local_sem=sem.sent)
+        sent += _bits(mk[kind])
+
+    if rank is None:
+        g.wait_ge(sem.sent, sent)
+        return
+
+    ps = [T.ps0, T.ps1, T.ps2, T.ps3]
+    nq = V // NQ
+    oc = 64 // NQ
+    gc = 4 * V // NQ
+
+    g.vector.wait_ge(sem.ldn, 128)
+    g.vector.tensor_copy(T.off[:], T.nbi[:]).then_inc(sem.offr, 1)
+
+    g.tensor.wait_ge(sem.ldw, 16)
+    g.tensor.wait_ge(sem.ldx, 16)
+    for q in range(NQ):
+        a = rank * V + q * nq
+        g.tensor.matmul(ps[q][:, 0:nq], T.wsb[:], T.win[:, a:a + nq], True, False)
+
+    for eng in (g.vector, g.scalar):
+        eng.wait_ge(sem.offr, 1)
+        eng.wait_ge(sem.ldx, 16)
+        for u in range(NR):
+            if u != rank:
+                eng.wait_ge(sem["a%d" % u], lands[u])
+    vq = [0, 1]
+    sq = [2, 3]
+    for q in vq:
+        g.vector.tensor_copy(T.gat[:, q * gc:(q + 1) * gc],
+                             T.win[:, 0:NR * V].indirect(T.off[:, q * oc:(q + 1) * oc])).then_inc(sem["g%d" % q], 1)
+    for q in sq:
+        g.scalar.activation(T.gat[:, q * gc:(q + 1) * gc],
+                            T.win[:, 0:NR * V].indirect(T.off[:, q * oc:(q + 1) * oc]),
+                            ActivationFunctionType.Copy).then_inc(sem["g%d" % q], 1)
+    for q in (vq[0], sq[0], vq[1], sq[1]):
+        g.tensor.wait_ge(sem["g%d" % q], 1)
+        for k in range(4):
+            mm = g.tensor.matmul(ps[q][:, 0:nq], T.wsb[:], T.gat[:, q * gc + k:(q + 1) * gc:4], False, k == 3)
+        mm.then_inc(sem["m%d" % q], 1)
+    for q in vq:
+        g.vector.wait_ge(sem["m%d" % q], 1)
+        g.vector.tensor_scalar(T.ysb[:, q * nq:(q + 1) * nq], ps[q][:, 0:nq], 0.0, None, AluOpType.max).then_inc(sem.rl, 1)
+    for q in sq:
+        g.scalar.wait_ge(sem["m%d" % q], 1)
+        g.scalar.activation(T.ysb[:, q * nq:(q + 1) * nq], ps[q][:, 0:nq], ActivationFunctionType.Relu).then_inc(sem.rl, 1)
+    g.sync.wait_ge(sem.rl, NQ)
+    g.sync.dma_start(T.y[:], T.ysb[:]).then_inc(sem.st, 16)
+    g.sync.wait_ge(sem.st, 16)
+    g.wait_ge(sem.sent, sent)

@@ -4,12 +4,12 @@ from concourse.mybir import AluOpType, ActivationFunctionType
 V = 256
 NR = 16
 NQ = 4
-ND = 2
-LIM = 7
+HOP = 3
 NSIM = 128
 
 SCRATCH = {
     "win": ("sbuf", [128, NR * V], "bfloat16"),
+    "rel": ("dram", [NR, 128, V], "bfloat16"),
     "wsb": ("sbuf", [128, 128], "bfloat16"),
     "nbi": ("sbuf", [128, 64], "int32"),
     "off": ("sbuf", [128, 64], "uint16"),
@@ -20,7 +20,7 @@ SCRATCH = {
     "ps2": ("psum", [128, 512], "float32"),
     "ps3": ("psum", [128, 512], "float32"),
 }
-SEMAPHORES = ["a%d" % u for u in range(NR)] + ["ldx", "ldw", "ldn", "offr", "sent", "rl", "st"] + \
+SEMAPHORES = ["a%d" % u for u in range(NR)] + ["ldx", "ldo", "ldw", "ldn", "offr", "sent", "rl", "st"] + \
              ["g%d" % q for q in range(NQ)] + ["m%d" % q for q in range(NQ)]
 
 
@@ -34,70 +34,64 @@ def make_plan(ranks, topo):
         if topo.chip(c) not in chips:
             chips.append(topo.chip(c))
     on = dict((ch, [c for c in ranks if topo.chip(c) == ch]) for ch in chips)
+    spare = dict((ch, [c for c in range(NSIM) if topo.chip(c) == ch and c not in ranks]) for ch in chips)
     unit = dict((c, i) for i, c in enumerate(ranks))
     n = len(chips)
 
-    def can(w, b):
-        return all(topo.may_write(w, d) for d in on[b])
+    def can(s, b):
+        return all(topo.may_write(s, d) for d in on[b] + spare[b])
 
-    first = {}
-    fwd = {}
-    steps = {}
+    jobs = {}
+    came = {}
+    aided = {}
     for i, a in enumerate(chips):
         others = [chips[(i + k) % n] for k in range(1, n)]
-        mine = on[a]
-        got = dict((w, []) for w in mine)
-        free = []
-        for o in mine:
-            for b in others:
-                able = [w for w in mine if can(w, b)]
-                if len(able) == 1:
-                    got[able[0]].append((o, b))
-                else:
-                    free.append((o, b))
-        free.sort(key=lambda t: len(got[t[0]]))
-        for o, b in free:
-            w = min(mine, key=lambda x: (len(got[x]), x != o))
-            got[w].append((o, b))
-        helpers = [c for c in range(NSIM) if topo.chip(c) == a and c not in ranks and all(can(c, b) for b in others)]
-        handed = dict((o, []) for o in mine)
-        for w in mine:
-            while len(got[w]) > LIM and helpers:
-                k = max(j for j, t in enumerate(got[w]) if t[0] != w)
-                o, b = got[w].pop(k)
-                h = helpers.pop()
-                handed[o].append(h)
-                steps[h] = [(unit[o], list(on[b]), "off")]
-        for w in mine:
-            own = [t for t in got[w] if t[0] == w]
-            oth = [t for t in got[w] if t[0] != w]
-            seq = own + oth
-            pos = 0
-            lists = {}
-            for j, (o, b) in enumerate(seq):
-                if o != w:
-                    pos = max(pos, 2)
-                if j >= len(seq) - ND:
-                    d = list(on[b])
-                    pos += len(d)
-                else:
-                    same = [r for r in on[b] if topo.die(r) == topo.die(w)]
-                    e = same[0] if same else on[b][0]
-                    d = [e]
-                    pos += 1
-                    fwd.setdefault(e, []).append((pos, unit[o]))
-                lists.setdefault(o, []).extend(d)
-            partners = [p for p in mine if p != w]
-            s_on = (unit[w], handed[w] + partners, "on")
-            s_off = (unit[w], lists.get(w, []), "off")
-            s = [s_on, s_off] if handed[w] else [s_off, s_on]
-            for o in mine:
-                if o != w and lists.get(o):
-                    s.append((unit[o], lists[o], "off"))
-            first[w] = [t for t in s if t[1]]
-    for w in ranks:
-        partners = [p for p in on[topo.chip(w)] if p != w]
-        steps[w] = first[w] + [(u, partners, "on") for _, u in sorted(fwd.get(w, []))]
+        for o in on[a]:
+            every = [h for h in spare[a] if all(can(h, b) for b in others) and h not in jobs]
+            aides = [h for h in every if topo.die(h) == topo.die(o)] or every
+            team = [o] + aides
+            load = dict((s, 0 if s == o else HOP) for s in team)
+            got = dict((s, []) for s in team)
+            order = sorted(others, key=lambda b: (len([s for s in team if can(s, b)]), others.index(b)))
+            for b in order:
+                s = min([t for t in team if can(t, b)], key=lambda t: (load[t], t != o))
+                load[s] += 1
+                got[s].append(b)
+            aided[o] = [h for h in aides if got[h]]
+            for s in team:
+                if not got[s]:
+                    continue
+                got[s].sort(key=others.index)
+                jobs[s] = (unit[o], got[s])
+                for j, b in enumerate(got[s]):
+                    t = (0 if s == o else HOP) + j + 1
+                    came.setdefault((b, topo.die(s)), []).append((t, others.index(b), unit[o], s))
+
+    relay = {}
+    work = {}
+    for (b, d), lst in came.items():
+        rs = [h for h in spare[b] if topo.die(h) == d] or spare[b]
+        rs = sorted(rs, key=lambda h: (h in jobs, h))
+        for j, (t, k, u, s) in enumerate(sorted(lst)):
+            h = rs[j % len(rs)]
+            relay[(u, b)] = h
+            work.setdefault(h, []).append(u)
+
+    steps = {}
+    for o in ranks:
+        u = unit[o]
+        st = []
+        if aided[o]:
+            st.append((u, aided[o], "on", "dram"))
+        if o in jobs:
+            st.append((u, [relay[(u, b)] for b in jobs[o][1]], "off", "dram"))
+        st.append((u, [p for p in on[topo.chip(o)] if p != o], "on", "sbuf"))
+        steps[o] = [t for t in st if t[1]]
+    for s, (u, bs) in jobs.items():
+        if s not in unit:
+            steps[s] = [(u, [relay[(u, b)] for b in bs], "off", "dram")]
+    for h, us in work.items():
+        steps.setdefault(h, []).extend((u, list(on[topo.chip(h)]), "all", "sbuf") for u in us)
     return steps
 
 
@@ -105,7 +99,7 @@ def masks(core, topo):
     far = [c for c in range(NSIM) if topo.chip(c) != topo.chip(core)][0]
     near = [c for c in range(NSIM) if topo.chip(c) == topo.chip(core) and c != core][0]
     off = topo.mask(core, far)
-    return {"off": off, "on": topo.mask(core, near) & ~off}
+    return {"off": off, "on": topo.mask(core, near) & ~off, "all": topo.mask(core, near)}
 
 
 def rank_program(g, core, T, topo):
@@ -119,7 +113,7 @@ def rank_program(g, core, T, topo):
     lands = {}
     for src, st in plan.items():
         mk = masks(src, topo)
-        for u, dsts, kind in st:
+        for u, dsts, kind, place in st:
             if core in dsts:
                 lands[u] = _bits(mk[kind])
 
@@ -127,7 +121,8 @@ def rank_program(g, core, T, topo):
         return T.win[:, u * V:(u + 1) * V]
 
     if rank is not None:
-        g.sync.dma_start(slot(rank), T.x[:]).then_inc(sem.ldx, 16)
+        g.sync.dma_start(T.rel[rank], T.x[:]).then_inc(sem.ldx, 16)
+        g.scalar.dma_start(slot(rank), T.x[:]).then_inc(sem.ldo, 16)
         g.scalar.dma_start(T.wsb[:], T.w[:]).then_inc(sem.ldw, 16)
         for k in range(8):
             q = g.sync if k % 2 == 0 else g.scalar
@@ -137,7 +132,7 @@ def rank_program(g, core, T, topo):
     mk = masks(core, topo)
     sent = 0
     waited = set()
-    for u, dsts, kind in plan[core]:
+    for u, dsts, kind, place in plan[core]:
         if u != rank and u not in waited:
             g.wait_ge(sem["a%d" % u], lands[u])
             waited.add(u)
@@ -146,7 +141,8 @@ def rank_program(g, core, T, topo):
             rid, pid, _ = topo.addr(d)
             ids.append(DstId(rid=rid, pnc=pid))
         t = RemoteDMATransfer(dst_ids=ids, dma_engine_mask=mk[kind], remote_sem=sem["a%d" % u],
-                              srcs=[slot(u)], dsts=[slot(u) for _ in dsts], alu_op=0)
+                              srcs=[T.rel[u]], dsts=[(T.rel[u] if place == "dram" else slot(u)) for _ in dsts],
+                              alu_op=0)
         g.remote_dma_fused([t], local_sem=sem.sent)
         sent += _bits(mk[kind])
 
@@ -163,35 +159,32 @@ def rank_program(g, core, T, topo):
     g.vector.tensor_copy(T.off[:], T.nbi[:]).then_inc(sem.offr, 1)
 
     g.tensor.wait_ge(sem.ldw, 16)
-    g.tensor.wait_ge(sem.ldx, 16)
+    g.tensor.wait_ge(sem.ldo, 16)
     for q in range(NQ):
         a = rank * V + q * nq
         g.tensor.matmul(ps[q][:, 0:nq], T.wsb[:], T.win[:, a:a + nq], True, False)
 
     for eng in (g.vector, g.scalar):
         eng.wait_ge(sem.offr, 1)
-        eng.wait_ge(sem.ldx, 16)
+        eng.wait_ge(sem.ldo, 16)
         for u in range(NR):
             if u != rank:
                 eng.wait_ge(sem["a%d" % u], lands[u])
-    vq = [0, 1]
-    sq = [2, 3]
-    for q in vq:
-        g.vector.tensor_copy(T.gat[:, q * gc:(q + 1) * gc],
-                             T.win[:, 0:NR * V].indirect(T.off[:, q * oc:(q + 1) * oc])).then_inc(sem["g%d" % q], 1)
-    for q in sq:
-        g.scalar.activation(T.gat[:, q * gc:(q + 1) * gc],
-                            T.win[:, 0:NR * V].indirect(T.off[:, q * oc:(q + 1) * oc]),
+    for q in range(NQ):
+        g.vector.tensor_copy(T.gat[:, q * gc:q * gc + gc // 2],
+                             T.win[:, 0:NR * V].indirect(T.off[:, q * oc:q * oc + oc // 2])).then_inc(sem["g%d" % q], 1)
+        g.scalar.activation(T.gat[:, q * gc + gc // 2:(q + 1) * gc],
+                            T.win[:, 0:NR * V].indirect(T.off[:, q * oc + oc // 2:(q + 1) * oc]),
                             ActivationFunctionType.Copy).then_inc(sem["g%d" % q], 1)
-    for q in (vq[0], sq[0], vq[1], sq[1]):
-        g.tensor.wait_ge(sem["g%d" % q], 1)
+    for q in range(NQ):
+        g.tensor.wait_ge(sem["g%d" % q], 2)
         for k in range(4):
             mm = g.tensor.matmul(ps[q][:, 0:nq], T.wsb[:], T.gat[:, q * gc + k:(q + 1) * gc:4], False, k == 3)
         mm.then_inc(sem["m%d" % q], 1)
-    for q in vq:
+    for q in (1, 3):
         g.vector.wait_ge(sem["m%d" % q], 1)
         g.vector.tensor_scalar(T.ysb[:, q * nq:(q + 1) * nq], ps[q][:, 0:nq], 0.0, None, AluOpType.max).then_inc(sem.rl, 1)
-    for q in sq:
+    for q in (0, 2):
         g.scalar.wait_ge(sem["m%d" % q], 1)
         g.scalar.activation(T.ysb[:, q * nq:(q + 1) * nq], ps[q][:, 0:nq], ActivationFunctionType.Relu).then_inc(sem.rl, 1)
     g.sync.wait_ge(sem.rl, NQ)

from concourse.bass import DstId, RemoteDMATransfer
from concourse.mybir import AluOpType, ActivationFunctionType

V = 256
NR = 16
NQ = 4
HOP = 3
NSIM = 128

SCRATCH = {
    "win": ("sbuf", [128, NR * V], "bfloat16"),
    "rel": ("dram", [NR, 128, V], "bfloat16"),
    "wsb": ("sbuf", [128, 128], "bfloat16"),
    "nbi": ("sbuf", [128, 64], "int32"),
    "off": ("sbuf", [128, 64], "uint16"),
    "gat": ("sbuf", [128, 4 * V], "bfloat16"),
    "ysb": ("sbuf", [128, V], "bfloat16"),
    "ps0": ("psum", [128, 512], "float32"),
    "ps1": ("psum", [128, 512], "float32"),
    "ps2": ("psum", [128, 512], "float32"),
    "ps3": ("psum", [128, 512], "float32"),
}
SEMAPHORES = ["a%d" % u for u in range(NR)] + ["ldx", "ldo", "ldw", "ldn", "offr", "sent", "rl", "st"] + \
             ["g%d" % q for q in range(NQ)] + ["m%d" % q for q in range(NQ)]


def _bits(m):
    return bin(m).count("1")


def make_plan(ranks, topo):
    chips = []
    for c in ranks:
        if topo.chip(c) not in chips:
            chips.append(topo.chip(c))
    on = dict((ch, [c for c in ranks if topo.chip(c) == ch]) for ch in chips)
    spare = dict((ch, [c for c in range(NSIM) if topo.chip(c) == ch and c not in ranks]) for ch in chips)
    unit = dict((c, i) for i, c in enumerate(ranks))
    n = len(chips)

    def can(s, b):
        return all(topo.may_write(s, d) for d in on[b] + spare[b])

    jobs = {}
    came = {}
    aided = {}
    for i, a in enumerate(chips):
        others = [chips[(i + k) % n] for k in range(1, n)]
        for o in on[a]:
            every = [h for h in spare[a] if all(can(h, b) for b in others) and h not in jobs]
            aides = [h for h in every if topo.die(h) == topo.die(o)] or every
            team = [o] + aides
            load = dict((s, 0 if s == o else HOP) for s in team)
            got = dict((s, []) for s in team)
            order = sorted(others, key=lambda b: (len([s for s in team if can(s, b)]), others.index(b)))
            for b in order:
                s = min([t for t in team if can(t, b)], key=lambda t: (load[t], t != o))
                load[s] += 1
                got[s].append(b)
            aided[o] = [h for h in aides if got[h]]
            for s in team:
                if not got[s]:
                    continue
                got[s].sort(key=others.index)
                jobs[s] = (unit[o], got[s])
                for j, b in enumerate(got[s]):
                    t = (0 if s == o else HOP) + j + 1
                    came.setdefault((b, topo.die(s)), []).append((t, others.index(b), unit[o], s))

    relay = {}
    work = {}
    for (b, d), lst in came.items():
        rs = [h for h in spare[b] if topo.die(h) == d] or spare[b]
        rs = sorted(rs, key=lambda h: (h in jobs, h))
        for j, (t, k, u, s) in enumerate(sorted(lst)):
            h = rs[j % len(rs)]
            relay[(u, b)] = h
            work.setdefault(h, []).append(u)

    steps = {}
    for o in ranks:
        u = unit[o]
        st = []
        if aided[o]:
            st.append((u, aided[o], "on", "dram"))
        if o in jobs:
            st.append((u, [relay[(u, b)] for b in jobs[o][1]], "off", "dram"))
        st.append((u, [p for p in on[topo.chip(o)] if p != o], "on", "sbuf"))
        steps[o] = [t for t in st if t[1]]
    for s, (u, bs) in jobs.items():
        if s not in unit:
            steps[s] = [(u, [relay[(u, b)] for b in bs], "off", "dram")]
    for h, us in work.items():
        steps.setdefault(h, []).extend((u, list(on[topo.chip(h)]), "all", "sbuf") for u in us)
    return steps


def masks(core, topo):
    far = [c for c in range(NSIM) if topo.chip(c) != topo.chip(core)][0]
    near = [c for c in range(NSIM) if topo.chip(c) == topo.chip(core) and c != core][0]
    off = topo.mask(core, far)
    return {"off": off, "on": topo.mask(core, near) & ~off, "all": topo.mask(core, near)}


def rank_program(g, core, T, topo):
    ranks = list(T.cores)
    plan = make_plan(ranks, topo)
    if core not in plan:
        return
    rank = T.rank_of(core)
    sem = T.sem

    lands = {}
    for src, st in plan.items():
        mk = masks(src, topo)
        for u, dsts, kind, place in st:
            if core in dsts:
                lands[u] = _bits(mk[kind])

    def slot(u):
        return T.win[:, u * V:(u + 1) * V]

    if rank is not None:
        g.sync.dma_start(T.rel[rank], T.x[:]).then_inc(sem.ldx, 16)
        g.scalar.dma_start(slot(rank), T.x[:]).then_inc(sem.ldo, 16)
        g.scalar.dma_start(T.wsb[:], T.w[:]).then_inc(sem.ldw, 16)
        for k in range(8):
            q = g.sync if k % 2 == 0 else g.scalar
            q.dma_start(T.nbi[16 * k:16 * k + 16, :], T.nb[:]).then_inc(sem.ldn, 16)
        g.wait_ge(sem.ldx, 16)

    mk = masks(core, topo)
    sent = 0
    waited = set()
    for u, dsts, kind, place in plan[core]:
        if u != rank and u not in waited:
            g.wait_ge(sem["a%d" % u], lands[u])
            waited.add(u)
        ids = []
        for d in dsts:
            rid, pid, _ = topo.addr(d)
            ids.append(DstId(rid=rid, pnc=pid))
        t = RemoteDMATransfer(dst_ids=ids, dma_engine_mask=mk[kind], remote_sem=sem["a%d" % u],
                              srcs=[T.rel[u]], dsts=[(T.rel[u] if place == "dram" else slot(u)) for _ in dsts],
                              alu_op=0)
        g.remote_dma_fused([t], local_sem=sem.sent)
        sent += _bits(mk[kind])

    if rank is None:
        g.wait_ge(sem.sent, sent)
        return

    ps = [T.ps0, T.ps1, T.ps2, T.ps3]
    nq = V // NQ
    oc = 64 // NQ
    gc = 4 * V // NQ

    g.vector.wait_ge(sem.ldn, 128)
    g.vector.tensor_copy(T.off[:], T.nbi[:]).then_inc(sem.offr, 1)

    g.tensor.wait_ge(sem.ldw, 16)
    g.tensor.wait_ge(sem.ldo, 16)
    for q in range(NQ):
        a = rank * V + q * nq
        g.tensor.matmul(ps[q][:, 0:nq], T.wsb[:], T.win[:, a:a + nq], True, False)

    for eng in (g.vector, g.scalar):
        eng.wait_ge(sem.offr, 1)
        eng.wait_ge(sem.ldo, 16)
        for u in range(NR):
            if u != rank:
                eng.wait_ge(sem["a%d" % u], lands[u])
    for q in range(NQ):
        g.vector.tensor_copy(T.gat[:, q * gc:q * gc + gc // 2],
                             T.win[:, 0:NR * V].indirect(T.off[:, q * oc:q * oc + oc // 2])).then_inc(sem["g%d" % q], 1)
        g.scalar.activation(T.gat[:, q * gc + gc // 2:(q + 1) * gc],
                            T.win[:, 0:NR * V].indirect(T.off[:, q * oc + oc // 2:(q + 1) * oc]),
                            ActivationFunctionType.Copy).then_inc(sem["g%d" % q], 1)
    for q in range(NQ):
        g.tensor.wait_ge(sem["g%d" % q], 2)
        for k in range(4):
            mm = g.tensor.matmul(ps[q][:, 0:nq], T.wsb[:], T.gat[:, q * gc + k:(q + 1) * gc:4], False, k == 3)
        mm.then_inc(sem["m%d" % q], 1)
    for q in (1, 3):
        g.vector.wait_ge(sem["m%d" % q], 1)
        g.vector.tensor_scalar(T.ysb[:, q * nq:(q + 1) * nq], ps[q][:, 0:nq], 0.0, None, AluOpType.max).then_inc(sem.rl, 1)
    for q in (0, 2):
        g.scalar.wait_ge(sem["m%d" % q], 1)
        g.scalar.activation(T.ysb[:, q * nq:(q + 1) * nq], ps[q][:, 0:nq], ActivationFunctionType.Relu).then_inc(sem.rl, 1)
    g.sync.wait_ge(sem.rl, NQ)
    g.sync.dma_start(T.y[:], T.ysb[:]).then_inc(sem.st, 16)
    g.sync.wait_ge(sem.st, 16)
    g.wait_ge(sem.sent, sent)
